import numpy as np
import ml_dtypes


def mxq(x, axis, fmt="e4m3"):
    dtype, down = {"e4m3": (ml_dtypes.float8_e4m3fn, 7), "e5m2": (ml_dtypes.float8_e5m2, 14)}[fmt]
    v = np.moveaxis(np.asarray(x, np.float32).astype(ml_dtypes.bfloat16).astype(np.float64), axis, -1)
    blocks = v.reshape(v.shape[:-1] + (-1, 32))
    amax = np.abs(blocks).max(-1, keepdims=True)
    byte = np.maximum(np.where(amax > 0, np.frexp(amax)[1] - 1 + 127, 0) - down, 1)
    scale = np.exp2(byte - 127.0)
    codes = (blocks / scale).astype(np.float32).astype(dtype).astype(np.float64)
    return np.moveaxis((codes * scale).reshape(v.shape), -1, axis)


WIDE = False


def mx_kscale(k):
    if not WIDE:
        return np.ones(k)
    levels = np.array([10, -10, 5, -5, 0])
    if k % 512:
        return np.exp2(np.random.permutation(np.resize(levels, k // 32))).repeat(32)
    a = np.empty((k // 512, 16))
    for p in range(k // 512):
        a[p, :8] = np.random.permutation(np.resize(levels, 8))
        for g in range(8):
            far = levels[np.abs(levels - a[p, g]) >= 10]
            a[p, g + 8] = far[np.random.randint(len(far))]
    return np.exp2(a.ravel()).repeat(32)


def f64(x):
    return np.asarray(x).astype(np.float64)


def striped(idx):
    return np.tile(idx.reshape(-1, 16).T, (8, 1)).astype(np.uint16)


def unstriped(offs):
    return offs[:16].T.reshape(-1).astype(np.int64)


def sigmoid(v):
    return 1.0 / (1.0 + np.exp(-np.maximum(v, -700.0)))


def gelu(v):
    return 0.5 * v * (1.0 + np.tanh(np.sqrt(2.0 / np.pi) * (v + 0.044715 * v**3)))

def planes(y):
    n, m = y.shape
    v = y.astype(np.float32).astype(ml_dtypes.bfloat16).astype(np.float64).reshape(n // 32, 32, m)
    top = np.abs(v).max(1)
    byte = np.clip(np.where(top > 0, np.frexp(top)[1] - 1 + 127 - 7, 1), 1, 254)
    codes = (v * np.exp2(127.0 - byte)[:, None, :]).reshape(n, m).astype(np.float32).astype(ml_dtypes.float8_e4m3fn).view(np.uint8)
    words = codes.reshape(n // 512, 128, 4, m).transpose(0, 1, 3, 2)
    return np.ascontiguousarray(words), np.ascontiguousarray(byte.astype(np.uint8).reshape(n // 512, 16, m))


K, T, S, N = 512, 1024, 512, 512


def setup_inputs():
    n = np.random.standard_normal
    s = mx_kscale(K)[:, None]
    return {
        "xT": (n((K, T)) * s).astype(np.float32),
        "res": n((N, T)).astype(np.float32),
        "w1": (n((K, N)) / np.sqrt(K) / s).astype(np.float32),
        "w2": (n((K, N)) / np.sqrt(K) / s).astype(np.float32),
        "offs": striped(np.random.permutation(T)[:S]),
    }


def reference(xT, res, w1, w2, offs):
    r = f64(res)[:, unstriped(offs)]
    xq = mxq(f64(xT)[:, unstriped(offs)], 0, "e4m3")
    g = sigmoid(mxq(f64(w2), 0, "e4m3").T @ xq)
    y = gelu(mxq(f64(w1), 0, "e4m3").T @ xq)
    out_0 = r + g * (y - r)
    return (out_0,) + planes(out_0)

@@ -1,0 +1,153 @@
+from contextlib import ExitStack
+
+import concourse.mybir as mybir
+
+F32 = mybir.dt.float32
+BF16 = mybir.dt.bfloat16
+I32 = mybir.dt.int32
+U32 = mybir.dt.uint32
+U16 = mybir.dt.uint16
+U8 = mybir.dt.uint8
+FP8X4 = mybir.dt.float8_e4m3fn_x4
+ACT = mybir.ActivationFunctionType
+ALU = mybir.AluOpType
+
+P = 128
+PACK = 4
+K, T, S, N = 512, 1024, 512, 512
+HALF = S // 2
+FLOPS = 2 * 2 * K * S * N
+
+
+def tile_picked_highway_gelu_lo_kernel(tc, xT, res, w1, w2, offs, out_0, out_1, out_2):
+    nc = tc.nc
+    with ExitStack() as ctx:
+        keep = ctx.enter_context(tc.tile_pool(name="keep", bufs=1))
+        psum = ctx.enter_context(tc.psum_pool(name="psum", bufs=1))
+
+        def sb(shape, dtype, name):
+            return keep.tile(shape, dtype, name=name, align_bytes=64)
+
+        def halves(h):
+            return slice(h * HALF, (h + 1) * HALF)
+
+        offsets = keep.tile([P, S // 16], U16, name="offsets")
+
+        def picked(window, lo, hi):
+            return window[:].indirect(offsets[:, lo // 16 : hi // 16])
+
+        x_rows = xT.rearrange("(p j) c -> p j c", j=PACK)
+        r_rows = res.rearrange("(p t) c -> p t c", t=PACK)
+        o_rows = out_0.rearrange("(p t) c -> p t c", t=PACK)
+        x_raw = [sb([P, T], F32, f"x_raw{j}") for j in range(PACK)]
+        r_raw = [sb([P, T], F32, f"r_raw{t}") for t in range(PACK)]
+        w_raw = [sb([P, PACK, N], F32, f"w_raw{i}") for i in range(2)]
+        nc.sync.dma_start(x_raw[0][:], x_rows[:, 0, :])
+        nc.sync.dma_start(offsets[:], offs)
+        for j in range(1, PACK):
+            nc.sync.dma_start(x_raw[j][:], x_rows[:, j, :])
+        for i, w in enumerate((w1, w2)):
+            nc.sync.dma_start(w_raw[i][:], w.rearrange("(p j) c -> p j c", j=PACK))
+        for t in range(PACK):
+            nc.sync.dma_start(r_raw[t][:], r_rows[:, t, :])
+
+        x_planes = sb([P, PACK * S], BF16, "x_planes")
+        x_woven = [sb([P, HALF * PACK], BF16, f"x_woven{h}") for h in range(2)]
+        x_codes = sb([P, S], U32, "x_codes")
+        x_scales = sb([P, S], U8, "x_scales")
+        for j in range(PACK - 1):
+            nc.scalar.activation(x_planes[:, j * S : (j + 1) * S], picked(x_raw[j], 0, S), ACT.Copy)
+        last = (PACK - 1) * S
+        nc.scalar.activation(x_planes[:, last : last + HALF], picked(x_raw[PACK - 1], 0, HALF), ACT.Copy)
+        nc.vector.tensor_copy(x_planes[:, last + HALF : last + S], picked(x_raw[PACK - 1], HALF, S))
+        x_view = x_planes[:].rearrange("p (j h c i) -> p h c j i", j=PACK, h=2, i=4)
+        for h in range(2):
+            nc.vector.tensor_copy(x_woven[h][:].rearrange("p (c i j) -> p c j i", i=4, j=PACK), x_view[:, h])
+
+        def quantise(codes, scales, values):
+            nc.vector.quantize_mx(out=codes.bitcast(FP8X4), scales=scales, in_=values)
+
+        w_woven = [[sb([P, 2 * P * PACK], BF16, f"w_woven{i}_{u}") for u in range(2)] for i in range(2)]
+        w_codes = [[sb([P, 2 * P], U32, f"w_codes{i}_{u}") for u in range(2)] for i in range(2)]
+        w_scales = [[sb([P, 2 * P], U8, f"w_scales{i}_{u}") for u in range(2)] for i in range(2)]
+
+        def deal(i, u):
+            dst = w_woven[i][u][:].rearrange("p (t m j) -> p m j t", t=2, j=PACK)
+            src = w_raw[i][:].rearrange("p j (m t) -> p m j t", t=PACK)[:, :, :, 2 * u : 2 * u + 2]
+            return dst, src
+
+        banks = [[psum.tile([P, S], F32, name=f"bank{i}_{t}") for t in range(PACK)] for i in range(2)]
+
+        def products(i, u):
+            quantise(w_codes[i][u][:], w_scales[i][u][:], w_woven[i][u][:])
+            for s in range(2):
+                cols = slice(s * P, (s + 1) * P)
+                nc.tensor.matmul_mx(
+                    out=banks[i][2 * u + s][:],
+                    lhsT=w_codes[i][u][:, cols].bitcast(FP8X4),
+                    lhsT_scale=w_scales[i][u][:, cols],
+                    rhs=x_codes[:].bitcast(FP8X4),
+                    rhs_scale=x_scales[:],
+                    start=True,
+                    stop=True,
+                )
+
+        y = [sb([P, 2, S], F32, f"y{u}") for u in range(2)]
+        gate = [sb([P, 2, S], F32, f"gate{u}") for u in range(2)]
+        diff = [sb([P, 2, S], F32, f"diff{u}") for u in range(2)]
+        r_pick = sb([P, 2, S], F32, "r_pick")
+        pull = [[sb([P, 2, HALF], F32, f"pull{u}_{h}") for h in range(2)] for u in range(2)]
+        result = [sb([P, PACK, HALF], F32, f"result{h}") for h in range(2)]
+
+        quantise(x_codes[:, halves(0)], x_scales[:, halves(0)], x_woven[0][:])
+        nc.vector.tensor_copy(*deal(0, 0))
+        nc.scalar.copy(*deal(0, 1))
+        quantise(x_codes[:, halves(1)], x_scales[:, halves(1)], x_woven[1][:])
+        for u in range(2):
+            products(0, u)
+        for t in range(PACK):
+            nc.scalar.activation(y[t // 2][:, t % 2, :], banks[0][t][:], ACT.Gelu_apprx_tanh)
+        for u in range(2):
+            nc.vector.tensor_copy(*deal(1, u))
+        for u in range(2):
+            products(1, u)
+
+        def gate_of(t):
+            nc.scalar.activation(gate[t // 2][:, t % 2, :], banks[1][t][:], ACT.Tanh, scale=-0.5)
+
+        def blend(u):
+            for h in range(2):
+                nc.vector.scalar_tensor_tensor(pull[u][h][:], gate[u][:, :, halves(h)], 1.0, diff[u][:, :, halves(h)], ALU.add, ALU.mult)
+            for h in range(2):
+                rows = result[h][:, 2 * u : 2 * u + 2, :]
+                nc.vector.scalar_tensor_tensor(rows, pull[u][h][:], 0.5, y[u][:, :, halves(h)], ALU.mult, ALU.add)
+                nc.sync.dma_start(o_rows[:, 2 * u : 2 * u + 2, halves(h)], rows)
+
+        for s in range(2):
+            nc.vector.tensor_tensor(diff[0][:, s, :], picked(r_raw[s], 0, S), y[0][:, s, :], ALU.subtract)
+            gate_of(s)
+        blend(0)
+        for s in range(2):
+            nc.scalar.activation(r_pick[:, s, :], picked(r_raw[2 + s], 0, S), ACT.Copy)
+            gate_of(2 + s)
+            nc.vector.tensor_tensor(diff[1][:, s, :], r_pick[:, s, :], y[1][:, s, :], ALU.subtract)
+        blend(1)
+
+        o_woven = [sb([P, HALF * PACK], BF16, f"o_woven{h}") for h in range(2)]
+        o_codes = sb([P, S], U32, "o_codes")
+        o_scales = sb([P, S], U8, "o_scales")
+        words = out_1[0].rearrange("p c r -> p (c r)").bitcast(I32)
+        scale_rows = out_2[0].bitcast(I32)
+
+        def weave(h):
+            dst = o_woven[h][:].rearrange("p (c i t) -> p c t i", i=4, t=PACK)
+            return dst, result[h][:].rearrange("p t (c i) -> p c t i", i=4)
+
+        nc.scalar.copy(*weave(0))
+        nc.vector.tensor_copy(*weave(1))
+        for h in range(2):
+            quantise(o_codes[:, halves(h)], o_scales[:, halves(h)], o_woven[h][:])
+        nc.sync.dma_start(words, o_codes[:].bitcast(I32))
+        for q in range(4):
+            queue = nc.sync if q == 3 else nc.scalar
+            queue.dma_start(scale_rows[4 * q : 4 * q + 4, :], o_scales[32 * q : 32 * q + 4, :].bitcast(I32))

@@ -16,6 +16,7 @@ P = 128
 PACK = 4
 K, T, S, N = 512, 1024, 512, 512
 HALF = S // 2
+FIRST = 64
 FLOPS = 2 * 2 * K * S * N
 
 
@@ -25,8 +26,8 @@ def tile_picked_highway_gelu_lo_kernel(tc, xT, res, w1, w2, offs, out_0, out_1, 
         keep = ctx.enter_context(tc.tile_pool(name="keep", bufs=1))
         psum = ctx.enter_context(tc.psum_pool(name="psum", bufs=1))
 
-        def sb(shape, dtype, name):
-            return keep.tile(shape, dtype, name=name, align_bytes=64)
+        def sb(shape, dtype, name, tag=None):
+            return keep.tile(shape, dtype, name=name, tag=tag or name, align_bytes=64)
 
         def halves(h):
             return slice(h * HALF, (h + 1) * HALF)
@@ -41,13 +42,14 @@ def tile_picked_highway_gelu_lo_kernel(tc, xT, res, w1, w2, offs, out_0, out_1, 
         o_rows = out_0.rearrange("(p t) c -> p t c", t=PACK)
         x_raw = [sb([P, T], F32, f"x_raw{j}") for j in range(PACK)]
         r_raw = [sb([P, T], F32, f"r_raw{t}") for t in range(PACK)]
-        w_raw = [sb([P, PACK, N], F32, f"w_raw{i}") for i in range(2)]
+        w_raw = [[sb([P, PACK, N // 2], F32, f"w_raw{i}_{c}") for c in range(2)] for i in range(2)]
         nc.sync.dma_start(x_raw[0][:], x_rows[:, 0, :])
         nc.sync.dma_start(offsets[:], offs)
         for j in range(1, PACK):
             nc.sync.dma_start(x_raw[j][:], x_rows[:, j, :])
         for i, w in enumerate((w1, w2)):
-            nc.sync.dma_start(w_raw[i][:], w.rearrange("(p j) c -> p j c", j=PACK))
+            for c in range(2):
+                nc.sync.dma_start(w_raw[i][c][:], w.rearrange("(p j) (c n) -> c p j n", j=PACK, c=2)[c])
         for t in range(PACK):
             nc.sync.dma_start(r_raw[t][:], r_rows[:, t, :])
 
@@ -55,8 +57,10 @@ def tile_picked_highway_gelu_lo_kernel(tc, xT, res, w1, w2, offs, out_0, out_1, 
         x_woven = [sb([P, HALF * PACK], BF16, f"x_woven{h}") for h in range(2)]
         x_codes = sb([P, S], U32, "x_codes")
         x_scales = sb([P, S], U8, "x_scales")
-        for j in range(PACK - 1):
-            nc.scalar.activation(x_planes[:, j * S : (j + 1) * S], picked(x_raw[j], 0, S), ACT.Copy)
+        nc.scalar.activation(x_planes[:, 0:FIRST], picked(x_raw[0], 0, FIRST), ACT.Copy)
+        nc.vector.tensor_copy(x_planes[:, FIRST:S], picked(x_raw[0], FIRST, S))
+        nc.vector.tensor_copy(x_planes[:, S : 2 * S], picked(x_raw[1], 0, S))
+        nc.scalar.activation(x_planes[:, 2 * S : 3 * S], picked(x_raw[2], 0, S), ACT.Copy)
         last = (PACK - 1) * S
         nc.scalar.activation(x_planes[:, last : last + HALF], picked(x_raw[PACK - 1], 0, HALF), ACT.Copy)
         nc.vector.tensor_copy(x_planes[:, last + HALF : last + S], picked(x_raw[PACK - 1], HALF, S))
@@ -71,53 +75,74 @@ def tile_picked_highway_gelu_lo_kernel(tc, xT, res, w1, w2, offs, out_0, out_1, 
         w_codes = [[sb([P, 2 * P], U32, f"w_codes{i}_{u}") for u in range(2)] for i in range(2)]
         w_scales = [[sb([P, 2 * P], U8, f"w_scales{i}_{u}") for u in range(2)] for i in range(2)]
 
-        def deal(i, u):
-            dst = w_woven[i][u][:].rearrange("p (t m j) -> p m j t", t=2, j=PACK)
-            src = w_raw[i][:].rearrange("p j (m t) -> p m j t", t=PACK)[:, :, :, 2 * u : 2 * u + 2]
+        def deal(i, c, u):
+            dst = w_woven[i][u][:].rearrange("p (t c m j) -> p c m j t", t=2, c=2, j=PACK)[:, c]
+            src = w_raw[i][c][:].rearrange("p j (m t) -> p m j t", t=PACK)[:, :, :, 2 * u : 2 * u + 2]
             return dst, src
 
         banks = [[psum.tile([P, S], F32, name=f"bank{i}_{t}") for t in range(PACK)] for i in range(2)]
 
-        def products(i, u):
+        def quantise_w(i, u):
             quantise(w_codes[i][u][:], w_scales[i][u][:], w_woven[i][u][:])
-            for s in range(2):
-                cols = slice(s * P, (s + 1) * P)
-                nc.tensor.matmul_mx(
-                    out=banks[i][2 * u + s][:],
-                    lhsT=w_codes[i][u][:, cols].bitcast(FP8X4),
-                    lhsT_scale=w_scales[i][u][:, cols],
-                    rhs=x_codes[:].bitcast(FP8X4),
-                    rhs_scale=x_scales[:],
-                    start=True,
-                    stop=True,
-                )
 
+        def product(out, i, t, tokens):
+            cols = slice((t % 2) * P, (t % 2 + 1) * P)
+            nc.tensor.matmul_mx(
+                out=out,
+                lhsT=w_codes[i][t // 2][:, cols].bitcast(FP8X4),
+                lhsT_scale=w_scales[i][t // 2][:, cols],
+                rhs=x_codes[:, tokens].bitcast(FP8X4),
+                rhs_scale=x_scales[:, tokens],
+                start=True,
+                stop=True,
+            )
+
+        everyone = slice(0, S)
         y = [sb([P, 2, S], F32, f"y{u}") for u in range(2)]
-        gate = [sb([P, 2, S], F32, f"gate{u}") for u in range(2)]
+        gate = sb([P, 2, S], F32, "gate")
+        late_gate = []
         diff = [sb([P, 2, S], F32, f"diff{u}") for u in range(2)]
         r_pick = sb([P, 2, S], F32, "r_pick")
         pull = [[sb([P, 2, HALF], F32, f"pull{u}_{h}") for h in range(2)] for u in range(2)]
         result = [sb([P, PACK, HALF], F32, f"result{h}") for h in range(2)]
 
         quantise(x_codes[:, halves(0)], x_scales[:, halves(0)], x_woven[0][:])
-        nc.vector.tensor_copy(*deal(0, 0))
-        nc.scalar.copy(*deal(0, 1))
         quantise(x_codes[:, halves(1)], x_scales[:, halves(1)], x_woven[1][:])
         for u in range(2):
-            products(0, u)
-        for t in range(PACK):
-            nc.scalar.activation(y[t // 2][:, t % 2, :], banks[0][t][:], ACT.Gelu_apprx_tanh)
+            nc.scalar.copy(*deal(0, 0, u))
+        nc.vector.tensor_copy(*deal(0, 1, 0))
+        nc.scalar.copy(*deal(0, 1, 1))
         for u in range(2):
-            nc.vector.tensor_copy(*deal(1, u))
+            quantise_w(0, u)
+        for c in range(2):
+            for u in range(2):
+                nc.vector.tensor_copy(*deal(1, c, u))
         for u in range(2):
-            products(1, u)
+            quantise_w(1, u)
 
-        def gate_of(t):
-            nc.scalar.activation(gate[t // 2][:, t % 2, :], banks[1][t][:], ACT.Tanh, scale=-0.5)
+        def layer(t):
+            product(banks[0][t][:], 0, t, everyone)
+            nc.scalar.activation(y[t // 2][:, t % 2, :], banks[0][t][:], ACT.Gelu_apprx_tanh)
+
+        for t in range(2):
+            layer(t)
+        for t in range(2):
+            product(banks[1][t][:], 1, t, everyone)
+            nc.scalar.activation(gate[:, t, :], banks[1][t][:], ACT.Tanh, scale=-0.5)
+        for t in range(2, PACK):
+            layer(t)
+        for h in range(2):
+            for s in range(2):
+                product(banks[1][2 + h][:, halves(s)], 1, 2 + s, halves(h))
+
+        def gate_at(u, h):
+            if u == 0:
+                return gate[:, :, halves(h)]
+            return late_gate[h][:].rearrange("p (s c) -> p s c", s=2)
 
         def blend(u):
             for h in range(2):
-                nc.vector.scalar_tensor_tensor(pull[u][h][:], gate[u][:, :, halves(h)], 1.0, diff[u][:, :, halves(h)], ALU.add, ALU.mult)
+                nc.vector.scalar_tensor_tensor(pull[u][h][:], gate_at(u, h), 1.0, diff[u][:, :, halves(h)], ALU.add, ALU.mult)
             for h in range(2):
                 rows = result[h][:, 2 * u : 2 * u + 2, :]
                 nc.vector.scalar_tensor_tensor(rows, pull[u][h][:], 0.5, y[u][:, :, halves(h)], ALU.mult, ALU.add)
@@ -125,12 +150,13 @@ def tile_picked_highway_gelu_lo_kernel(tc, xT, res, w1, w2, offs, out_0, out_1, 
 
         for s in range(2):
             nc.vector.tensor_tensor(diff[0][:, s, :], picked(r_raw[s], 0, S), y[0][:, s, :], ALU.subtract)
-            gate_of(s)
         blend(0)
         for s in range(2):
             nc.scalar.activation(r_pick[:, s, :], picked(r_raw[2 + s], 0, S), ACT.Copy)
-            gate_of(2 + s)
             nc.vector.tensor_tensor(diff[1][:, s, :], r_pick[:, s, :], y[1][:, s, :], ALU.subtract)
+        for h in range(2):
+            late_gate.append(sb([P, S], F32, f"late_gate{h}", tag=f"r_raw{2 + h}"))
+            nc.scalar.activation(late_gate[h][:], banks[1][2 + h][:], ACT.Tanh, scale=-0.5)
         blend(1)
 
         o_woven = [sb([P, HALF * PACK], BF16, f"o_woven{h}") for h in range(2)]
@@ -139,15 +165,18 @@ def tile_picked_highway_gelu_lo_kernel(tc, xT, res, w1, w2, offs, out_0, out_1, 
         words = out_1[0].rearrange("p c r -> p (c r)").bitcast(I32)
         scale_rows = out_2[0].bitcast(I32)
 
-        def weave(h):
-            dst = o_woven[h][:].rearrange("p (c i t) -> p c t i", i=4, t=PACK)
-            return dst, result[h][:].rearrange("p t (c i) -> p c t i", i=4)
+        def weave(h, u):
+            pair = slice(2 * u, 2 * u + 2)
+            dst = o_woven[h][:].rearrange("p (c t) -> p c t", t=PACK)[:, :, pair]
+            return dst, result[h][:, pair, :].rearrange("p t c -> p c t")
 
-        nc.scalar.copy(*weave(0))
-        nc.vector.tensor_copy(*weave(1))
+        for h in range(2):
+            nc.scalar.copy(*weave(h, 0))
+        nc.scalar.copy(*weave(0, 1))
+        nc.vector.tensor_copy(*weave(1, 1))
         for h in range(2):
             quantise(o_codes[:, halves(h)], o_scales[:, halves(h)], o_woven[h][:])
-        nc.sync.dma_start(words, o_codes[:].bitcast(I32))
+            nc.sync.dma_start(words[:, halves(h)], o_codes[:, halves(h)].bitcast(I32))
         for q in range(4):
             queue = nc.sync if q == 3 else nc.scalar
             queue.dma_start(scale_rows[4 * q : 4 * q + 4, :], o_scales[32 * q : 32 * q + 4, :].bitcast(I32))

@@ -148,18 +148,22 @@ def tile_picked_highway_gelu_lo_kernel(tc, xT, res, w1, w2, offs, out_0, out_1, 
                 nc.vector.scalar_tensor_tensor(rows, pull[u][h][:], 0.5, y[u][:, :, halves(h)], ALU.mult, ALU.add)
                 nc.sync.dma_start(o_rows[:, 2 * u : 2 * u + 2, halves(h)], rows)
 
-        for s in range(2):
-            nc.vector.tensor_tensor(diff[0][:, s, :], picked(r_raw[s], 0, S), y[0][:, s, :], ALU.subtract)
+        nc.vector.tensor_tensor(diff[0][:, 0, :], picked(r_raw[0], 0, S), y[0][:, 0, :], ALU.subtract)
+        for h in range(2):
+            looked_up = picked(r_raw[1], h * HALF, (h + 1) * HALF)
+            nc.vector.tensor_tensor(diff[0][:, 1, halves(h)], looked_up, y[0][:, 1, halves(h)], ALU.subtract)
         blend(0)
         for s in range(2):
             nc.scalar.activation(r_pick[:, s, :], picked(r_raw[2 + s], 0, S), ACT.Copy)
-            nc.vector.tensor_tensor(diff[1][:, s, :], r_pick[:, s, :], y[1][:, s, :], ALU.subtract)
+        nc.vector.tensor_tensor(diff[1][:, 0, :], r_pick[:, 0, :], y[1][:, 0, :], ALU.subtract)
+        for h in range(2):
+            nc.vector.tensor_tensor(diff[1][:, 1, halves(h)], r_pick[:, 1, halves(h)], y[1][:, 1, halves(h)], ALU.subtract)
         for h in range(2):
             late_gate.append(sb([P, S], F32, f"late_gate{h}", tag=f"r_raw{2 + h}"))
             nc.scalar.activation(late_gate[h][:], banks[1][2 + h][:], ACT.Tanh, scale=-0.5)
         blend(1)
 
-        o_woven = [sb([P, HALF * PACK], BF16, f"o_woven{h}") for h in range(2)]
+        o_woven = sb([P, 2, HALF * PACK], BF16, "o_woven", tag="r_pick")
         o_codes = sb([P, S], U32, "o_codes")
         o_scales = sb([P, S], U8, "o_scales")
         words = out_1[0].rearrange("p c r -> p (c r)").bitcast(I32)
@@ -167,7 +171,7 @@ def tile_picked_highway_gelu_lo_kernel(tc, xT, res, w1, w2, offs, out_0, out_1, 
 
         def weave(h, u):
             pair = slice(2 * u, 2 * u + 2)
-            dst = o_woven[h][:].rearrange("p (c t) -> p c t", t=PACK)[:, :, pair]
+            dst = o_woven[:, h, :].rearrange("p (c t) -> p c t", t=PACK)[:, :, pair]
             return dst, result[h][:, pair, :].rearrange("p t c -> p c t")
 
         for h in range(2):
@@ -175,7 +179,7 @@ def tile_picked_highway_gelu_lo_kernel(tc, xT, res, w1, w2, offs, out_0, out_1, 
         nc.scalar.copy(*weave(0, 1))
         nc.vector.tensor_copy(*weave(1, 1))
         for h in range(2):
-            quantise(o_codes[:, halves(h)], o_scales[:, halves(h)], o_woven[h][:])
+            quantise(o_codes[:, halves(h)], o_scales[:, halves(h)], o_woven[:, h, :])
             nc.sync.dma_start(words[:, halves(h)], o_codes[:, halves(h)].bitcast(I32))
         for q in range(4):
             queue = nc.sync if q == 3 else nc.scalar

from contextlib import ExitStack

import concourse.mybir as mybir

F32 = mybir.dt.float32
BF16 = mybir.dt.bfloat16
I32 = mybir.dt.int32
U32 = mybir.dt.uint32
U16 = mybir.dt.uint16
U8 = mybir.dt.uint8
FP8X4 = mybir.dt.float8_e4m3fn_x4
ACT = mybir.ActivationFunctionType
ALU = mybir.AluOpType

P = 128
PACK = 4
K, T, S, N = 512, 1024, 512, 512
HALF = S // 2
FIRST = 64
FLOPS = 2 * 2 * K * S * N


def tile_picked_highway_gelu_lo_kernel(tc, xT, res, w1, w2, offs, out_0, out_1, out_2):
    nc = tc.nc
    with ExitStack() as ctx:
        keep = ctx.enter_context(tc.tile_pool(name="keep", bufs=1))
        psum = ctx.enter_context(tc.psum_pool(name="psum", bufs=1))

        def sb(shape, dtype, name, tag=None):
            return keep.tile(shape, dtype, name=name, tag=tag or name, align_bytes=64)

        def halves(h):
            return slice(h * HALF, (h + 1) * HALF)

        offsets = keep.tile([P, S // 16], U16, name="offsets")

        def picked(window, lo, hi):
            return window[:].indirect(offsets[:, lo // 16 : hi // 16])

        x_rows = xT.rearrange("(p j) c -> p j c", j=PACK)
        r_rows = res.rearrange("(p t) c -> p t c", t=PACK)
        o_rows = out_0.rearrange("(p t) c -> p t c", t=PACK)
        x_raw = [sb([P, T], F32, f"x_raw{j}") for j in range(PACK)]
        r_raw = [sb([P, T], F32, f"r_raw{t}") for t in range(PACK)]
        w_raw = [[sb([P, PACK, N // 2], F32, f"w_raw{i}_{c}") for c in range(2)] for i in range(2)]
        nc.sync.dma_start(x_raw[0][:], x_rows[:, 0, :])
        nc.sync.dma_start(offsets[:], offs)
        for j in range(1, PACK):
            nc.sync.dma_start(x_raw[j][:], x_rows[:, j, :])
        for i, w in enumerate((w1, w2)):
            for c in range(2):
                nc.sync.dma_start(w_raw[i][c][:], w.rearrange("(p j) (c n) -> c p j n", j=PACK, c=2)[c])
        for t in range(PACK):
            nc.sync.dma_start(r_raw[t][:], r_rows[:, t, :])

        x_planes = sb([P, PACK * S], BF16, "x_planes")
        x_woven = [sb([P, HALF * PACK], BF16, f"x_woven{h}") for h in range(2)]
        x_codes = sb([P, S], U32, "x_codes")
        x_scales = sb([P, S], U8, "x_scales")
        nc.scalar.activation(x_planes[:, 0:FIRST], picked(x_raw[0], 0, FIRST), ACT.Copy)
        nc.vector.tensor_copy(x_planes[:, FIRST:S], picked(x_raw[0], FIRST, S))
        nc.vector.tensor_copy(x_planes[:, S : 2 * S], picked(x_raw[1], 0, S))
        nc.scalar.activation(x_planes[:, 2 * S : 3 * S], picked(x_raw[2], 0, S), ACT.Copy)
        last = (PACK - 1) * S
        nc.scalar.activation(x_planes[:, last : last + HALF], picked(x_raw[PACK - 1], 0, HALF), ACT.Copy)
        nc.vector.tensor_copy(x_planes[:, last + HALF : last + S], picked(x_raw[PACK - 1], HALF, S))
        x_view = x_planes[:].rearrange("p (j h c i) -> p h c j i", j=PACK, h=2, i=4)
        for h in range(2):
            nc.vector.tensor_copy(x_woven[h][:].rearrange("p (c i j) -> p c j i", i=4, j=PACK), x_view[:, h])

        def quantise(codes, scales, values):
            nc.vector.quantize_mx(out=codes.bitcast(FP8X4), scales=scales, in_=values)

        w_woven = [[sb([P, 2 * P * PACK], BF16, f"w_woven{i}_{u}") for u in range(2)] for i in range(2)]
        w_codes = [[sb([P, 2 * P], U32, f"w_codes{i}_{u}") for u in range(2)] for i in range(2)]
        w_scales = [[sb([P, 2 * P], U8, f"w_scales{i}_{u}") for u in range(2)] for i in range(2)]

        def deal(i, c, u):
            dst = w_woven[i][u][:].rearrange("p (t c m j) -> p c m j t", t=2, c=2, j=PACK)[:, c]
            src = w_raw[i][c][:].rearrange("p j (m t) -> p m j t", t=PACK)[:, :, :, 2 * u : 2 * u + 2]
            return dst, src

        banks = [[psum.tile([P, S], F32, name=f"bank{i}_{t}") for t in range(PACK)] for i in range(2)]

        def quantise_w(i, u):
            quantise(w_codes[i][u][:], w_scales[i][u][:], w_woven[i][u][:])

        def product(out, i, t, tokens):
            cols = slice((t % 2) * P, (t % 2 + 1) * P)
            nc.tensor.matmul_mx(
                out=out,
                lhsT=w_codes[i][t // 2][:, cols].bitcast(FP8X4),
                lhsT_scale=w_scales[i][t // 2][:, cols],
                rhs=x_codes[:, tokens].bitcast(FP8X4),
                rhs_scale=x_scales[:, tokens],
                start=True,
                stop=True,
            )

        everyone = slice(0, S)
        y = [sb([P, 2, S], F32, f"y{u}") for u in range(2)]
        gate = sb([P, 2, S], F32, "gate")
        late_gate = []
        diff = [sb([P, 2, S], F32, f"diff{u}") for u in range(2)]
        r_pick = sb([P, 2, S], F32, "r_pick")
        pull = [[sb([P, 2, HALF], F32, f"pull{u}_{h}") for h in range(2)] for u in range(2)]
        result = [sb([P, PACK, HALF], F32, f"result{h}") for h in range(2)]

        quantise(x_codes[:, halves(0)], x_scales[:, halves(0)], x_woven[0][:])
        quantise(x_codes[:, halves(1)], x_scales[:, halves(1)], x_woven[1][:])
        for u in range(2):
            nc.scalar.copy(*deal(0, 0, u))
        nc.vector.tensor_copy(*deal(0, 1, 0))
        nc.scalar.copy(*deal(0, 1, 1))
        for u in range(2):
            quantise_w(0, u)
        for c in range(2):
            for u in range(2):
                nc.vector.tensor_copy(*deal(1, c, u))
        for u in range(2):
            quantise_w(1, u)

        def layer(t):
            product(banks[0][t][:], 0, t, everyone)
            nc.scalar.activation(y[t // 2][:, t % 2, :], banks[0][t][:], ACT.Gelu_apprx_tanh)

        for t in range(2):
            layer(t)
        for t in range(2):
            product(banks[1][t][:], 1, t, everyone)
            nc.scalar.activation(gate[:, t, :], banks[1][t][:], ACT.Tanh, scale=-0.5)
        for t in range(2, PACK):
            layer(t)
        for h in range(2):
            for s in range(2):
                product(banks[1][2 + h][:, halves(s)], 1, 2 + s, halves(h))

        def gate_at(u, h):
            if u == 0:
                return gate[:, :, halves(h)]
            return late_gate[h][:].rearrange("p (s c) -> p s c", s=2)

        def blend(u):
            for h in range(2):
                nc.vector.scalar_tensor_tensor(pull[u][h][:], gate_at(u, h), 1.0, diff[u][:, :, halves(h)], ALU.add, ALU.mult)
            for h in range(2):
                rows = result[h][:, 2 * u : 2 * u + 2, :]
                nc.vector.scalar_tensor_tensor(rows, pull[u][h][:], 0.5, y[u][:, :, halves(h)], ALU.mult, ALU.add)
                nc.sync.dma_start(o_rows[:, 2 * u : 2 * u + 2, halves(h)], rows)

        nc.vector.tensor_tensor(diff[0][:, 0, :], picked(r_raw[0], 0, S), y[0][:, 0, :], ALU.subtract)
        for h in range(2):
            looked_up = picked(r_raw[1], h * HALF, (h + 1) * HALF)
            nc.vector.tensor_tensor(diff[0][:, 1, halves(h)], looked_up, y[0][:, 1, halves(h)], ALU.subtract)
        blend(0)
        for s in range(2):
            nc.scalar.activation(r_pick[:, s, :], picked(r_raw[2 + s], 0, S), ACT.Copy)
        nc.vector.tensor_tensor(diff[1][:, 0, :], r_pick[:, 0, :], y[1][:, 0, :], ALU.subtract)
        for h in range(2):
            nc.vector.tensor_tensor(diff[1][:, 1, halves(h)], r_pick[:, 1, halves(h)], y[1][:, 1, halves(h)], ALU.subtract)
        for h in range(2):
            late_gate.append(sb([P, S], F32, f"late_gate{h}", tag=f"r_raw{2 + h}"))
            nc.scalar.activation(late_gate[h][:], banks[1][2 + h][:], ACT.Tanh, scale=-0.5)
        blend(1)

        o_woven = sb([P, 2, HALF * PACK], BF16, "o_woven", tag="r_pick")
        o_codes = sb([P, S], U32, "o_codes")
        o_scales = sb([P, S], U8, "o_scales")
        words = out_1[0].rearrange("p c r -> p (c r)").bitcast(I32)
        scale_rows = out_2[0].bitcast(I32)

        def weave(h, u):
            pair = slice(2 * u, 2 * u + 2)
            dst = o_woven[:, h, :].rearrange("p (c t) -> p c t", t=PACK)[:, :, pair]
            return dst, result[h][:, pair, :].rearrange("p t c -> p c t")

        for h in range(2):
            nc.scalar.copy(*weave(h, 0))
        nc.scalar.copy(*weave(0, 1))
        nc.vector.tensor_copy(*weave(1, 1))
        for h in range(2):
            quantise(o_codes[:, halves(h)], o_scales[:, halves(h)], o_woven[:, h, :])
            nc.sync.dma_start(words[:, halves(h)], o_codes[:, halves(h)].bitcast(I32))
        for q in range(4):
            queue = nc.sync if q == 3 else nc.scalar
            queue.dma_start(scale_rows[4 * q : 4 * q + 4, :], o_scales[32 * q : 32 * q + 4, :].bitcast(I32))
